import numpy as np, ml_dtypes
CORES = [13,21,141,149]
N = 4
BF = ml_dtypes.bfloat16
T, R, S, H, CAP = 512, 64, 9, 4096, 2048
U, A, M, B0 = T // R, CAP // 16, max(T, CAP // 4), ((H + 1) << S) // 8191 + 1
def keys(x, hc):
    X = np.ascontiguousarray(x.transpose(1, 0, 2)).reshape(128, N * T).astype(np.int64); h = hc[0].astype(np.int64)
    before = np.concatenate([np.zeros((128, 1), np.int64), X[:, :-1]], axis=1)
    return X, ((h[:, :1] * before + h[:, 1:] * X) >> S) & (H - 1)
def stretches(v):
    return np.ascontiguousarray(v.reshape(128, N, T).transpose(1, 0, 2)).astype(np.float32)
def multipliers(rng):
    return np.stack([rng.integers(1, 1024, 128), rng.integers(B0, (1 << S) + 1, 128)], axis=1)
def keyset(rng, n):
    return np.argsort(rng.random((128, n)), axis=-1)[:, :M]
def pools(rng, K):
    return np.take_along_axis(np.broadcast_to(K, (N,) + K.shape), np.argsort(rng.random((N,) + K.shape), axis=-1), axis=-1)
def counts(rng):
    d = rng.integers(0, A - R + 1, (N, 64)); return np.stack([A + d, A - d], axis=2).reshape(N, 128)
def uneven(rng, n):
    v = np.concatenate([[T], R + n // 15 + (np.arange(15) < n % 15)])
    return rng.permuted(np.broadcast_to(v, (N, 8, 16)).copy(), axis=-1).reshape(N, 128)
def order(rng, D, P, pin=False):
    i = np.arange(P.shape[-1]); e = rng.random((N, 128, U, P.shape[-1]), dtype=np.float32)
    b = rng.permuted(np.broadcast_to(np.arange(U), (N, 128, U)).copy(), axis=-1)[..., None]
    e = e - (i // R == b) + 4 * (i >= D[:, :, None, None])
    if pin: e[..., 0] = -9; e[..., 1] = -8
    o = np.argsort(e, axis=-1)[..., :R]
    if pin: o = np.concatenate([o[..., :1], rng.permuted(o[..., 2:], axis=-1), o[..., 1:2]], axis=-1)
    else: o = rng.permuted(o, axis=-1)
    return np.take_along_axis(np.broadcast_to(P[:, :, None], (N, 128, U, P.shape[-1])), o, axis=-1).reshape(N, 128, T)
def spell(rng, k, h):
    kk = k.transpose(1, 0, 2).reshape(128, N * T).astype(np.int64); X = np.zeros((128, N * T), np.int64); coin = rng.random((128, N * T)); up = rng.random((128, N * T)) < 0.5; last = np.zeros(128, np.int64); a, b = h[:, 0], h[:, 1]
    for t in range(N * T):
        w = ((kk[:, t] << S) - a * last) & ((H << S) - 1); w2 = w + (H << S)
        w = np.where(up[:, t] & ((w2 + (1 << S) - 1) // b <= 8191), w2, w); lo = (w + b - 1) // b; hi = (w + (1 << S) - 1) // b
        last = lo + np.floor(coin[:, t] * (hi - lo + 1)).astype(np.int64); X[:, t] = last
    return {"x": np.ascontiguousarray(X.reshape(128, N, T).transpose(1, 0, 2)).astype(np.int32), "hc": np.broadcast_to(h, (N, 128, 2)).astype(np.int32)}
def setup_inputs(rng):
    D = np.maximum(R, counts(rng) - rng.integers(0, 5, (N, 128)))
    return spell(rng, order(rng, D, pools(rng, keyset(rng, H))), multipliers(rng))
def setup_inputs_full(rng):
    D = np.where(np.arange(128) // 16 % 2 == 0, uneven(rng, CAP - T - 15 * R), counts(rng))
    P = pools(rng, keyset(rng, H)); P[:, ::3] = np.stack([keyset(rng, H)[::3] for r in range(N)])
    return spell(rng, order(rng, D, P), multipliers(rng))
def setup_inputs_ends(rng):
    P = pools(rng, keyset(rng, H - 2) + 1); P[..., 0] = 0; P[..., 1] = H - 1
    k = order(rng, counts(rng), P, True).reshape(N, 128, U, R); k[:, ::2, 1::2, 0] = H - 1; k[:, ::2, 1::2, R - 1] = 0
    k[0, 1::4, 0, R - 1] = k[0, 1::4, 0, 1]; k[0, 1::4, 0, 0] = H - 1; k[0, 1::4, 0, 1] = 0
    h = multipliers(rng); h[1::4, 0] = 0
    d = spell(rng, k.reshape(N, 128, T), h); d["x"][0, 1::4, 1] = 0; return d
def setup_inputs_far(rng):
    K = keyset(rng, H); P = pools(rng, K[:, M // 2:]); Q = pools(rng, K[:, :M // 2]); P[0] = Q[0]; P[N - 1] = Q[N - 1]; P[N - 1, ::2] = Q[0, ::2]
    D = counts(rng); D[N - 1] = D[0]
    return spell(rng, order(rng, D, P), multipliers(rng))
def setup_inputs_same(rng):
    K = keyset(rng, H); k = order(rng, np.full((N, 128), R), np.broadcast_to(K, (N,) + K.shape))
    k[:, 1::2] = np.tile(k[0, 1::2, :R], (1, U)); return spell(rng, k, multipliers(rng))
def setup_inputs_spread(rng):
    K = (rng.integers(0, H, (128, 1)) + np.arange(M)) % H
    h = np.stack([rng.choice(np.array([0, 1, 1023]), 128), rng.choice(np.array([B0, 1 << S]), 128)], axis=1)
    return spell(rng, order(rng, uneven(rng, 0), pools(rng, K)), h)
def check_inputs(d):
    bad = []; x, hc = d["x"], d["hc"]
    if not (x.min() >= 0 and x.max() <= 8191): bad.append("tokens")
    if not (hc[..., 0].min() >= 0 and hc[..., 0].max() <= 1023 and hc[..., 1].min() >= 1 and hc[..., 1].max() <= 1 << S): bad.append("multipliers")
    if (hc != hc[:1]).any(): bad.append("hc_alike")
    k = keys(x, hc)[1].reshape(128, N, T).transpose(1, 0, 2)
    s = np.sort(k.reshape(N, 128, U, R), axis=-1)
    if (s[..., 1:] == s[..., :-1]).any(): bad.append("runs")
    s = np.sort(k, axis=-1); n = 1 + np.sum(s[..., 1:] != s[..., :-1], axis=-1)
    if np.sum(n.reshape(N, 8, 16), axis=-1).max() > CAP: bad.append("new_keys")
    return bad
def reference(x, hc):
    X, k = keys(x, hc); L = N * T
    u = (np.arange(128)[:, None] * H + k).reshape(-1); o = np.argsort(u, kind="stable")
    same = u[o[1:]] == u[o[:-1]]
    prev = np.full(128 * L, -1, np.int64); prev[o[1:][same]] = o[:-1][same] % L
    prev = prev.reshape(128, L); after = np.where(prev >= 0, np.take_along_axis(X, prev + 1, axis=1), -1)
    return {"y": stretches(prev), "z": stretches(after)}

@@ -1,0 +1,426 @@
+from concourse.bass import DstId, RemoteDMATransfer
+from concourse.mybir import AluOpType, ActivationFunctionType
+
+OFF = 32.0
+NONE = OFF - 1.0
+MAGIC = 12582912.0
+H = 4096
+MOVED = 768
+
+SCRATCH = {
+    "xd": ("dram", [8, 128, 64], "int32"),
+    "rin": ("dram", [128, 64], "int32"),
+    "rfull": ("dram", [128, 256], "float32"),
+    "rhalf": ("dram", [128, 128], "float32"),
+    "rfin": ("dram", [128, 128], "float32"),
+    "snd": ("dram", [3, 128, 256], "float32"),
+    "sndh": ("dram", [128, 128], "float32"),
+    "ldf": ("dram", [3, 128, 128], "float32"),
+    "land": ("sbuf", [128, 8, 64], "int32"),
+    "xf": ("sbuf", [128, 10, 64], "float32"),
+    "ta": ("sbuf", [128, 8, 64], "float32"),
+    "mix": ("sbuf", [128, 16, 32], "float32"),
+    "turn": ("sbuf", [128, 16, 32], "float32"),
+    "ki": ("sbuf", [128, 512], "int32"),
+    "w": ("sbuf", [128, 512], "uint16"),
+    "hci": ("sbuf", [128, 2], "int32"),
+    "hcf": ("sbuf", [128, 2], "float32"),
+    "hcs": ("sbuf", [128, 4], "float32"),
+    "ones": ("sbuf", [128, 128], "float32"),
+    "sh": ("sbuf", [128, 128], "float32"),
+    "wr": ("sbuf", [128, 128], "float32"),
+    "sel0": ("sbuf", [128, 128], "float32"),
+    "sel1": ("sbuf", [128, 128], "float32"),
+    "lift": ("sbuf", [128, 136], "float32"),
+    "tab0": ("sbuf", [128, H], "float32"),
+    "tab1": ("sbuf", [128, H], "float32"),
+    "tab2": ("sbuf", [128, H], "float32"),
+    "tab3": ("sbuf", [128, H], "float32"),
+    "val": ("sbuf", [128, 4, 2064], "float32"),
+    "got": ("sbuf", [128, 16, 512], "float32"),
+    "ld": ("sbuf", [128, 4, 256], "float32"),
+    "sndf": ("sbuf", [128, 128], "float32"),
+    "phc": ("psum", [128, 512], "float32"),
+    "pb0": ("psum", [128, 512], "float32"),
+    "pb1": ("psum", [128, 512], "float32"),
+    "ptb": ("psum", [128, 512], "float32"),
+    "px0": ("psum", [128, 512], "float32"),
+    "px1": ("psum", [128, 512], "float32"),
+}
+SEMAPHORES = ["copied", "hcin", "arr0", "arr1", "left", "rl_in", "rl_full", "rl_half", "rl_fin",
+              "ones", "t0a", "t0b", "vinit", "hcf", "hcp", "hcs", "sfa", "sfb", "sfc",
+              "gsel", "gsh", "gshw", "glift", "io0", "io1", "io2", "io3", "pt0", "pt1", "pt2",
+              "c1a", "c1b", "pba", "pbb", "prep", "w0", "w1", "rv0", "rv1", "rv2", "rv3",
+              "ch0", "ch1", "ch2", "ch3", "out0", "out1", "out2", "out3", "ldin", "ldfin",
+              "px0", "px1", "rnd", "rnd2", "sty", "stz"]
+
+
+def bits(engines):
+    m = 0
+    for e in engines:
+        m |= 1 << e
+    return m
+
+
+def helpers(T, topo, r):
+    me = T.cores[r]
+    far = [q for q in range(len(T.cores)) if q != r and not topo.may_write(me, T.cores[q])]
+    able = [c for c in topo.cores_of(me) if T.rank_of(c) is None and all(topo.may_write(c, T.cores[q]) for q in far)]
+    able.sort(key=lambda c: (topo.die(c) != topo.die(me), c))
+    out = {}
+    for e in range(2):
+        for n, q in enumerate(far):
+            out[(q, e)] = able[e * len(far) + n]
+    return out
+
+
+def helper_program(g, core, T, topo, r, q, e):
+    S = T.sem
+    dst = T.cores[q]
+    rid, pid = topo.addr(dst, core)
+    m = topo.mask(core, dst)
+    n = len(topo.engines(core, dst))
+    chip = len(topo.engines(T.cores[r], core))
+    g.wait_ge(S.rl_in, chip // 8)
+    g.remote_dma(T.land[:, 2 * r + e, :], T.rin[:], S.arr0 if r == 0 else S.arr1, S.left, pid, rid, m)
+    sent = n
+    if e == 0:
+        if q < 3:
+            g.wait_ge(S.rl_full, chip // 2)
+            g.remote_dma(T.ld[:, r, :], T.rfull[:], S.ldin, S.left, pid, rid, m)
+            sent += n
+        else:
+            g.wait_ge(S.rl_half, chip // 2)
+            g.remote_dma(T.ld[:, r, 0:128], T.rhalf[:], S.ldin, S.left, pid, rid, m)
+            g.wait_ge(S.rl_fin, chip)
+            g.remote_dma(T.ldf[r], T.rfin[:], S.ldfin, S.left, pid, rid, m)
+            sent += 2 * n
+    g.wait_ge(S.left, sent)
+
+
+def rank_program(g, core, T, topo):
+    N = len(T.cores)
+    rank = T.rank_of(core)
+    if rank is None:
+        for r in range(N):
+            for (q, e), c in helpers(T, topo, r).items():
+                if c == core:
+                    helper_program(g, core, T, topo, r, q, e)
+        return
+    S = T.sem
+    V, A, P, Y = g.vector, g.scalar, g.tensor, g.sync
+    q = rank
+    hel = helpers(T, topo, q)
+    near = [r for r in range(N) if r != q and (r, 0) not in hel]
+    Alu, Act = AluOpType, ActivationFunctionType
+    tabs = [T.tab0, T.tab1, T.tab2, T.tab3]
+    ch = [S.ch0, S.ch1, S.ch2, S.ch3]
+    rv = [S.rv0, S.rv1, S.rv2, S.rv3]
+    io = [S.io0, S.io1, S.io2, S.io3]
+    pt = [S.pt0, S.pt1, S.pt2]
+    outs = [S.out0, S.out1, S.out2, S.out3]
+
+    def lands(r):
+        src = T.cores[r] if topo.may_write(T.cores[r], core) else helpers(T, topo, r)[(q, 0)]
+        return len(topo.engines(src, core))
+
+    def slots_in(r):
+        if r == q:
+            return 32
+        return lands(r) if topo.may_write(T.cores[r], core) else 2 * lands(r)
+
+    def got_at(s, U):
+        r, u = U // 8, U % 8
+        if r < 3:
+            return T.got[:, 4 * r + s, 64 * u:64 * u + 64]
+        c = 256 * (s % 2) + 64 * (u % 4)
+        return T.got[:, 12 + 2 * (u // 4) + s // 2, c:c + 64]
+
+    arr0 = slots_in(0)
+    arr1 = sum(slots_in(r) for r in range(1, N))
+    ldin = 64 + sum(lands(r) for r in range(N) if r != q)
+
+    Y.dma_start(T.xd[:], T.x[:]).then_inc(S.copied, 16)
+    Y.dma_start(T.hci[:], T.hc[:]).then_inc(S.hcin, 16)
+    for e in range(2):
+        Y.dma_start(T.land[:, 2 * q + e, :], T.x[32 * q + 16 * e:32 * q + 16 * e + 16, :]).then_inc(S.arr0 if q == 0 else S.arr1, 16)
+
+    def tokens_to_rows(r):
+        Y.wait_ge(io[r], 1)
+        for e in range(2):
+            Y.dma_start(T.val[16 * e + 8:128:32, r, 0:2048], T.xf[:, 2 * r + 2 + e, :]).then_inc(rv[r], 16)
+
+    def answers_out(r):
+        runs = 8 if r < 3 else 4
+        for s in range(4):
+            Y.wait_ge(ch[s], 2 * (8 * r + runs - 1))
+        for row in range(2):
+            for e in range(2):
+                a0 = 64 * row + 32 * e
+                src = T.got[16 * e + 8 * row:128:32, 4 * r:4 * r + runs // 2, :]
+                if r == q:
+                    Y.dma_start(T.ld[a0:a0 + 32, q, 0:32 * runs], src).then_inc(S.ldin, 16)
+                elif r < 3:
+                    Y.dma_start(T.snd[r, a0:a0 + 32, :], src).then_inc(outs[r], 16)
+                else:
+                    Y.dma_start(T.sndh[a0:a0 + 32, :], src).then_inc(outs[r], 16)
+
+    Y.wait_ge(S.c1a, 1)
+    tokens_to_rows(0)
+    Y.wait_ge(S.c1b, 1)
+    tokens_to_rows(1)
+    tokens_to_rows(2)
+    answers_out(0)
+    tokens_to_rows(3)
+    for r in range(1, 4):
+        answers_out(r)
+    wide = 512 if q < 3 else 256
+    ny = nz = 0
+    if q == 3:
+        Y.wait_ge(S.rnd, 2)
+        Y.dma_start(T.y[96:128, 256:512], T.sndf[0:64, :]).then_inc(S.sty, 16)
+        Y.dma_start(T.z[96:128, 256:512], T.sndf[64:128, :]).then_inc(S.sty, 16)
+        ny += 32
+    Y.wait_ge(S.rnd2, 1)
+    for r in range(N):
+        Y.dma_start(T.y[32 * r:32 * r + 32, 0:wide], T.ld[0:64, r, 0:wide // 2]).then_inc(S.sty, 16)
+        ny += 16
+    fin = sum(lands(r) for r in range(3)) if q == 3 else 0
+    if q == 3:
+        Y.wait_ge(S.ldfin, fin)
+        Y.dma_start(T.y[0:96, 256:512], T.ldf[:, 0:64, :]).then_inc(S.sty, 16)
+        ny += 16
+    Y.wait_ge(S.sty, ny)
+
+    g.wait_ge(S.ones, 1)
+    for e, sel in enumerate((T.sel0, T.sel1)):
+        g.affine_select(sel[:], T.ones[:], [[-1, 16], [0, 8]], Alu.is_equal, 0.0, -(32 * q + 16 * e), 1).then_inc(S.gsel, 1)
+    g.affine_select(T.sh[:], T.ones[:], [[-1, 128]], Alu.is_equal, 0.0, 1, 1).then_inc(S.gsh, 1)
+    left = 0
+    g.wait_ge(S.copied, 16)
+    trs = []
+    for n, ((r, e), c) in enumerate(sorted(hel.items())):
+        eng = topo.engines(core, c)
+        k = len(eng) // 8
+        use = eng[len(eng) // 2 + n * k:len(eng) // 2 + (n + 1) * k]
+        rid, pid = topo.addr(c, core)
+        trs.append(RemoteDMATransfer(dst_ids=[DstId(rid=rid, pnc=pid)], dma_engine_mask=bits(use), remote_sem=S.rl_in,
+                                     src=T.xd[2 * r + e], dst=T.rin[:]))
+        left += k
+    g.remote_dma_fused(trs, local_sem=S.left)
+    for r in near:
+        c = T.cores[r]
+        eng = topo.engines(core, c)
+        k = len(eng) // 2
+        rid, pid = topo.addr(c, core)
+        trs = [RemoteDMATransfer(dst_ids=[DstId(rid=rid, pnc=pid)], dma_engine_mask=bits(eng[e * k:(e + 1) * k]),
+                                 remote_sem=S.arr0 if q == 0 else S.arr1, src=T.xd[2 * r + e], dst=T.land[:, 2 * q + e, :])
+               for e in range(2)]
+        g.remote_dma_fused(trs, local_sem=S.left)
+        left += 2 * k
+    g.affine_select(T.wr[:], T.ones[:], [[-8, 16], [1000, 8]], Alu.is_equal, 0.0, -7, 1).then_inc(S.gshw, 1)
+    g.wait_ge(S.gsh, 1)
+    g.iota(T.sh[:, 0:128:8], [[0, 16]], 0, 0, allow_small_or_imprecise_dtypes=True).then_inc(S.gshw, 1)
+    for r in range(4):
+        g.iota(T.val[:, r, 0:2048], [[0, 4], [1, 512]], 512 * r - 1 + int(OFF), 0,
+               allow_small_or_imprecise_dtypes=True).then_inc(io[r], 1)
+    for row in range(2):
+        g.affine_select(T.lift[:, 64 * row:64 * row + 64], T.ones[:, 0:64], [[-16, 2], [-32, 4], [1000, 8]],
+                        Alu.is_equal, 0.0, -8 * row - 7000, 1).then_inc(S.glift, 1)
+    for r in range(4):
+        if r == q:
+            continue
+        g.wait_ge(outs[r], 64)
+        src = T.snd[r] if r < 3 else T.sndh[:]
+        if r in near:
+            c = T.cores[r]
+            rid, pid = topo.addr(c, core)
+            g.remote_dma(T.ld[:, q, :] if r < 3 else T.ld[:, q, 0:128], src, S.ldin, S.left, pid, rid, topo.mask(core, c))
+            left += len(topo.engines(core, c))
+        else:
+            c = hel[(r, 0)]
+            eng = topo.engines(core, c)
+            use = eng[len(eng) // 2:]
+            rid, pid = topo.addr(c, core)
+            g.remote_dma(T.rfull[:] if r < 3 else T.rhalf[:], src, S.rl_full if r < 3 else S.rl_half, S.left, pid, rid, bits(use))
+            left += len(use)
+    if q != 3:
+        g.wait_ge(S.rnd, 2)
+        c = T.cores[3] if 3 in near else hel[(3, 0)]
+        rid, pid = topo.addr(c, core)
+        if 3 in near:
+            g.remote_dma(T.ldf[q], T.sndf[:], S.ldfin, S.left, pid, rid, topo.mask(core, c))
+        else:
+            g.remote_dma(T.rfin[:], T.sndf[:], S.rl_fin, S.left, pid, rid, topo.mask(core, c))
+        left += len(topo.engines(core, c))
+    g.wait_ge(S.left, left)
+
+    P.wait_ge(S.gsel, 2)
+    P.wait_ge(S.hcf, 1)
+    P.matmul(T.phc[:, 0:2], T.sel0[:], T.hcf[:], True, True).then_inc(S.hcp, 1)
+    P.matmul(T.phc[:, 2:4], T.sel1[:], T.hcf[:], True, True).then_inc(S.hcp, 1)
+    P.wait_ge(S.gshw, 2)
+    for r0, r1, pb, c1, done in ((0, 1, T.pb0, S.c1a, S.pba), (1, 4, T.pb1, S.c1b, S.pbb)):
+        P.wait_ge(c1, 1)
+        n = 2 * (r1 - r0)
+        P.matmul(pb[:, 0:n], T.sh[:], T.xf[:, 2 * r0 + 2:2 * r1 + 2, 63], True, False)
+        P.matmul(pb[:, 0:n], T.wr[:], T.xf[:, 2 * r0:2 * r1, 63], False, True).then_inc(done, 1)
+    P.wait_ge(S.glift, 2)
+    for U in range(28, 32):
+        wv, half = (U - 28) // 2, U % 2
+        px = (T.px0, T.px1)[half]
+        for n, s in enumerate((0, 2, 1, 3)):
+            P.wait_ge(ch[s], 2 * U)
+            j = 2 * s + wv
+            last = wv == 1 and n == 3
+            mm = P.matmul(px[:, 0:64], T.lift[:, 7 - j:135 - j], got_at(s, U), wv == 0 and n == 0, last)
+            if last:
+                mm.then_inc((S.px0, S.px1)[half], 1)
+
+    def offsets(s, U):
+        c = 128 * (U // 8) + 4 * (8 * s + U % 8)
+        return T.w[:, c:c + 4]
+
+    def walk(E, chains, gather, scatter, between):
+        for U in range(32):
+            if U == 8:
+                E.wait_ge(S.w1, 1)
+            if U > 0:
+                for s in chains:
+                    E.wait_ge(ch[s], 2 * U - 1)
+                    gather(got_at(s, U), tabs[s][:].indirect(offsets(s, U))).then_inc(ch[s], 1)
+                    between(U)
+            if U < 31:
+                if U % 8 == 7:
+                    E.wait_ge(pt[U // 8], 1)
+                for s in chains:
+                    if U > 0:
+                        E.wait_ge(ch[s], 2 * U)
+                    c = 512 * s + 64 * (U % 8) + 1
+                    scatter(tabs[s][:].indirect(offsets(s, U)), T.val[:, U // 8, c:c + 64]).then_inc(ch[s], 1)
+                    between(U)
+
+    A.wait_ge(S.t0a, 1)
+    A.activation(T.tab2[:, 0:512], T.tab0[:, 0:512], Act.Silu).then_inc(S.sfa, 1)
+    A.wait_ge(S.t0b, 1)
+    A.activation(T.tab2[:, 512:2560], T.tab0[:, 0:2048], Act.Identity).then_inc(S.sfa, 1)
+    A.activation(T.tab1[:, H - MOVED:H], T.tab0[:, 0:MOVED], Act.Identity).then_inc(S.sfa, 1)
+    A.wait_ge(S.sfa, 3)
+    A.activation(T.tab2[:, 2560:H], T.tab2[:, 0:H - 2560], Act.Identity).then_inc(S.sfc, 1)
+    A.activation(T.tab3[:, 0:2048], T.tab2[:, 0:2048], Act.Identity).then_inc(S.sfc, 1)
+    A.activation(T.tab3[:, 2048:H], T.tab2[:, 0:2048], Act.Identity).then_inc(S.sfc, 1)
+    A.wait_ge(S.sfc, 3)
+    A.wait_ge(S.w0, 1)
+    A.wait_ge(rv[0], 32)
+    walk(A, (2, 3), lambda o, i: A.activation(o, i, Act.Identity), lambda o, i: A.activation(o, i, Act.Silu), lambda U: None)
+    A.wait_ge(S.rnd2, 1)
+    for r in range(N):
+        A.dma_start(T.z[32 * r:32 * r + 32, 0:wide], T.ld[64:128, r, 0:wide // 2]).then_inc(S.stz, 16)
+        nz += 16
+    if q == 3:
+        A.wait_ge(S.ldfin, fin)
+        A.dma_start(T.z[0:96, 256:512], T.ldf[:, 64:128, :]).then_inc(S.stz, 16)
+        nz += 16
+    A.wait_ge(S.stz, nz)
+
+    prep = [0]
+
+    def stages(r0, r1, pb, c1, pbdone, wdone, arr, narr):
+        n = r1 - r0
+
+        def count(ins):
+            ins.then_inc(S.prep, 1)
+            prep[0] += 1
+
+        def tokens():
+            V.wait_ge(arr, narr)
+            V.tensor_scalar(T.xf[:, 2 * r0 + 2:2 * r1 + 2, :], T.land[:, 2 * r0:2 * r1, :], OFF, None, Alu.add).then_inc(c1, 1)
+
+        def products():
+            V.wait_ge(c1, 1)
+            for e in range(2):
+                x = T.xf[:, 2 * r0 + 2 + e:2 * r1 + 2:2, :]
+                count(V.tensor_scalar(T.ptb[:, 256 * e + 64 * r0:256 * e + 64 * r1], x, -OFF, T.hcs[:, 2 * e + 1:2 * e + 2], Alu.add, Alu.mult))
+                count(V.tensor_scalar(T.ta[:, 4 * e + r0:4 * e + r1, 1:64], T.xf[:, 2 * r0 + 2 + e:2 * r1 + 2:2, 0:63],
+                                      -OFF, T.hcs[:, 2 * e:2 * e + 1], Alu.add, Alu.mult))
+
+        def firsts():
+            V.wait_ge(pbdone, 1)
+            for e in range(2):
+                count(V.tensor_scalar(T.ta[:, 4 * e + r0:4 * e + r1, 0], pb[:, e:2 * n:2], -OFF, T.hcs[:, 2 * e:2 * e + 1], Alu.add, Alu.mult))
+
+        def sums():
+            V.wait_ge(S.prep, prep[0])
+            for e in range(2):
+                count(V.tensor_tensor(T.mix[:, 4 * r0:4 * r1, 16 * e:16 * e + 16], T.ta[:, 4 * e + r0:4 * e + r1, :],
+                                      T.ptb[:, 256 * e + 64 * r0:256 * e + 64 * r1], Alu.add))
+
+        def turn():
+            V.wait_ge(S.prep, prep[0])
+            count(V.transpose(T.turn[:, 4 * r0:4 * r1, :], T.mix[:, 4 * r0:4 * r1, :]))
+
+        def whole():
+            V.wait_ge(S.prep, prep[0])
+            for b in range(4):
+                count(V.tensor_copy(T.ki[:, 128 * r0 + b:128 * r1:4], T.turn[:, 4 * r0 + b:4 * r1:4, :]))
+
+        def key():
+            V.wait_ge(S.prep, prep[0])
+            k = T.ki[:, 128 * r0:128 * r1]
+            count(V.tensor_scalar(k, k, 9, H - 1, Alu.arith_shift_right, Alu.bitwise_and))
+
+        def narrow():
+            V.wait_ge(S.prep, prep[0])
+            V.tensor_copy(T.w[:, 128 * r0:128 * r1], T.ki[:, 128 * r0:128 * r1]).then_inc(wdone, 1)
+
+        return [tokens, products, firsts, sums, turn, whole, key, narrow]
+
+    def seam(r):
+        V.wait_ge(rv[r + 1], 32)
+        if r > 0:
+            V.wait_ge(pt[r - 1], 1)
+        V.tensor_copy(T.val[:, r, 512:2049:512], T.val[:, r + 1, 0:2048:512]).then_inc(pt[r], 1)
+
+    first = stages(0, 1, T.pb0, S.c1a, S.pba, S.w0, S.arr0, arr0)
+    rest = stages(1, 4, T.pb1, S.c1b, S.pbb, S.w1, S.arr1, arr1)
+    early = q == 0 or 0 in near
+
+    V.memset(T.ones[:], 1.0).then_inc(S.ones, 1)
+    V.memset(T.tab0[:, 0:512], NONE).then_inc(S.t0a, 1)
+    V.memset(T.tab0[:, 512:2048], NONE).then_inc(S.t0b, 1)
+    V.memset(T.xf[:, 0:2, :], OFF).then_inc(S.vinit, 1)
+    V.memset(T.got[:, 0:4, 0:64], NONE).then_inc(S.vinit, 1)
+    V.memset(T.lift[:, 128:136], 0.0).then_inc(S.vinit, 1)
+    V.memset(T.tab0[:, 2048:H], NONE).then_inc(S.vinit, 1)
+    V.wait_ge(S.hcin, 16)
+    V.tensor_copy(T.hcf[:], T.hci[:]).then_inc(S.hcf, 1)
+    V.memset(T.tab1[:, 0:2048], NONE).then_inc(S.vinit, 1)
+    V.wait_ge(S.hcp, 2)
+    V.tensor_copy(T.hcs[:], T.phc[:, 0:4]).then_inc(S.hcs, 1)
+    V.wait_ge(S.vinit, 5)
+    if early:
+        first[0]()
+    V.memset(T.tab1[:, 2048:H - MOVED], NONE).then_inc(S.sfb, 1)
+    if not early:
+        first[0]()
+    V.wait_ge(S.hcs, 1)
+    for step in first[1:]:
+        step()
+    V.wait_ge(S.sfb, 1)
+    V.wait_ge(S.sfa, 3)
+    V.wait_ge(S.w0, 1)
+    V.wait_ge(rv[0], 32)
+    seams = [0, 1, 2]
+
+    def between(U):
+        if rest:
+            rest.pop(0)()
+        elif seams and U >= (3, 12, 20)[seams[0]]:
+            seam(seams.pop(0))
+
+    walk(V, (0, 1), V.tensor_copy, V.tensor_copy, between)
+    for half, (px, sem) in enumerate(((T.px0, S.px0), (T.px1, S.px1))):
+        V.wait_ge(sem, 1)
+        V.tensor_scalar(T.sndf[:, 64 * half:64 * half + 64], px[:, 0:64], MAGIC - OFF, MAGIC, Alu.add, Alu.subtract).then_inc(S.rnd, 1)
+    V.wait_ge(S.ldin, ldin)
+    V.tensor_scalar(T.ld[:, :, 0:wide // 2], T.ld[:, :, 0:wide // 2], MAGIC - OFF, MAGIC, Alu.add, Alu.subtract).then_inc(S.rnd2, 1)

@@ -1,11 +1,15 @@
 from concourse.bass import DstId, RemoteDMATransfer
 from concourse.mybir import AluOpType, ActivationFunctionType
 
-OFF = 32.0
+OFF = 512.0
 NONE = OFF - 1.0
 MAGIC = 12582912.0
 H = 4096
-MOVED = 768
+BY_V, BY_G = 6400, 1024
+BY_A = (7168, 2 * H)
+GAP = ((384, 768, 256, 256, 256, 256), (384, 768, 0, 0, 0, 0))
+REST = (0, 4, 20, 21, 22, 23)
+SEAMS = (24, 56, 88)
 
 SCRATCH = {
     "xd": ("dram", [8, 128, 64], "int32"),
@@ -17,25 +21,21 @@ SCRATCH = {
     "sndh": ("dram", [128, 128], "float32"),
     "ldf": ("dram", [3, 128, 128], "float32"),
     "land": ("sbuf", [128, 8, 64], "int32"),
-    "xf": ("sbuf", [128, 10, 64], "float32"),
-    "ta": ("sbuf", [128, 8, 64], "float32"),
-    "mix": ("sbuf", [128, 16, 32], "float32"),
+    "xf": ("sbuf", [128, 10, 68], "float32"),
     "turn": ("sbuf", [128, 16, 32], "float32"),
     "ki": ("sbuf", [128, 512], "int32"),
     "w": ("sbuf", [128, 512], "uint16"),
-    "hci": ("sbuf", [128, 2], "int32"),
-    "hcf": ("sbuf", [128, 2], "float32"),
-    "hcs": ("sbuf", [128, 4], "float32"),
+    "hci": ("sbuf", [128, 2, 2], "int32"),
+    "hcf": ("sbuf", [128, 4], "float32"),
     "ones": ("sbuf", [128, 128], "float32"),
     "sh": ("sbuf", [128, 128], "float32"),
     "wr": ("sbuf", [128, 128], "float32"),
-    "sel0": ("sbuf", [128, 128], "float32"),
-    "sel1": ("sbuf", [128, 128], "float32"),
+    "sel": ("sbuf", [128, 128], "float32"),
+    "eye": ("sbuf", [128, 128], "float32"),
+    "diag": ("sbuf", [128, 4, 128], "float32"),
     "lift": ("sbuf", [128, 136], "float32"),
-    "tab0": ("sbuf", [128, H], "float32"),
-    "tab1": ("sbuf", [128, H], "float32"),
-    "tab2": ("sbuf", [128, H], "float32"),
-    "tab3": ("sbuf", [128, H], "float32"),
+    "tabv": ("sbuf", [128, 2 * H], "float32"),
+    "taba": ("sbuf", [128, 2 * H], "float32"),
     "val": ("sbuf", [128, 4, 2064], "float32"),
     "got": ("sbuf", [128, 16, 512], "float32"),
     "ld": ("sbuf", [128, 4, 256], "float32"),
@@ -43,14 +43,15 @@ SCRATCH = {
     "phc": ("psum", [128, 512], "float32"),
     "pb0": ("psum", [128, 512], "float32"),
     "pb1": ("psum", [128, 512], "float32"),
-    "ptb": ("psum", [128, 512], "float32"),
+    "pm0": ("psum", [128, 16, 32], "float32"),
+    "pm1": ("psum", [128, 16, 32], "float32"),
     "px0": ("psum", [128, 512], "float32"),
     "px1": ("psum", [128, 512], "float32"),
 }
-SEMAPHORES = ["copied", "hcin", "arr0", "arr1", "left", "rl_in", "rl_full", "rl_half", "rl_fin",
-              "ones", "t0a", "t0b", "vinit", "hcf", "hcp", "hcs", "sfa", "sfb", "sfc",
-              "gsel", "gsh", "gshw", "glift", "io0", "io1", "io2", "io3", "pt0", "pt1", "pt2",
-              "c1a", "c1b", "pba", "pbb", "prep", "w0", "w1", "rv0", "rv1", "rv2", "rv3",
+SEMAPHORES = ["copied", "copiedn", "sent", "gwr", "hcin", "arr0", "arr1", "left", "rl_in", "rl_full", "rl_half", "rl_fin",
+              "ones", "t0a", "t0b", "t0c", "back", "gfill", "io0a", "vinit", "vfill", "hcf", "hcp", "diag", "sfa", "sfc",
+              "gsel", "geye", "gsh", "gshw", "glift", "io0", "io1", "io2", "io3", "pt0", "pt1", "pt2",
+              "c1a", "c1b", "pba", "pbb", "bfa", "bfb", "pma", "pmb", "prep", "w0", "w1", "rv0", "rv1", "rv2", "rv3",
               "ch0", "ch1", "ch2", "ch3", "out0", "out1", "out2", "out3", "ldin", "ldfin",
               "px0", "px1", "rnd", "rnd2", "sty", "stz"]
 
@@ -113,7 +114,7 @@ def rank_program(g, core, T, topo):
     hel = helpers(T, topo, q)
     near = [r for r in range(N) if r != q and (r, 0) not in hel]
     Alu, Act = AluOpType, ActivationFunctionType
-    tabs = [T.tab0, T.tab1, T.tab2, T.tab3]
+    tabs = [T.tabv[:, 0:H], T.tabv[:, H:2 * H], T.taba[:, 0:H], T.taba[:, H:2 * H]]
     ch = [S.ch0, S.ch1, S.ch2, S.ch3]
     rv = [S.rv0, S.rv1, S.rv2, S.rv3]
     io = [S.io0, S.io1, S.io2, S.io3]
@@ -136,19 +137,27 @@ def rank_program(g, core, T, topo):
         c = 256 * (s % 2) + 64 * (u % 4)
         return T.got[:, 12 + 2 * (u // 4) + s // 2, c:c + 64]
 
+    late = 0 if q == 0 or 0 in near else 1
+    gap, by_a = GAP[late], BY_A[late]
+    back = 32 if by_a < 2 * H else 16
     arr0 = slots_in(0)
     arr1 = sum(slots_in(r) for r in range(1, N))
     ldin = 64 + sum(lands(r) for r in range(N) if r != q)
 
-    Y.dma_start(T.xd[:], T.x[:]).then_inc(S.copied, 16)
-    Y.dma_start(T.hci[:], T.hc[:]).then_inc(S.hcin, 16)
+    far = [r for r in range(N) if (r, 0) in hel]
+    for E, r in zip((Y, A), far):
+        E.dma_start(T.xd[2 * r:2 * r + 2], T.x[32 * r:32 * r + 32, :]).then_inc(S.copied, 16)
+    for r in near:
+        Y.dma_start(T.xd[2 * r:2 * r + 2], T.x[32 * r:32 * r + 32, :]).then_inc(S.copiedn, 16)
+    for e in range(2):
+        Y.dma_start(T.hci[0:16, e, :], T.hc[32 * q + 16 * e:32 * q + 16 * e + 16, :]).then_inc(S.hcin, 16)
     for e in range(2):
         Y.dma_start(T.land[:, 2 * q + e, :], T.x[32 * q + 16 * e:32 * q + 16 * e + 16, :]).then_inc(S.arr0 if q == 0 else S.arr1, 16)
 
     def tokens_to_rows(r):
-        Y.wait_ge(io[r], 1)
+        Y.wait_ge(io[r], 1 if r else 48)
         for e in range(2):
-            Y.dma_start(T.val[16 * e + 8:128:32, r, 0:2048], T.xf[:, 2 * r + 2 + e, :]).then_inc(rv[r], 16)
+            Y.dma_start(T.val[16 * e + 8:128:32, r, 0:2048], T.xf[:, 2 * r + 2 + e, 4:68]).then_inc(rv[r], 16)
 
     def answers_out(r):
         runs = 8 if r < 3 else 4
@@ -165,6 +174,15 @@ def rank_program(g, core, T, topo):
                 else:
                     Y.dma_start(T.sndh[a0:a0 + 32, :], src).then_inc(outs[r], 16)
 
+    if q == 0:
+        Y.wait_ge(S.sent, 1)
+    Y.wait_ge(S.io0a, 1)
+    for s in range(1, 4):
+        Y.dma_start(T.val[:, 0, 512 * s:512 * s + 512], T.val[:, 0, 0:512]).then_inc(io[0], 16)
+    Y.wait_ge(S.t0c, 1)
+    if by_a < 2 * H:
+        Y.dma_start(T.taba[:, by_a:2 * H], T.tabv[:, 0:2 * H - by_a]).then_inc(S.back, 16)
+    Y.dma_start(T.tabv[:, BY_V + BY_G:2 * H], T.tabv[:, 0:2 * H - BY_V - BY_G]).then_inc(S.back, 16)
     Y.wait_ge(S.c1a, 1)
     tokens_to_rows(0)
     Y.wait_ge(S.c1b, 1)
@@ -192,12 +210,11 @@ def rank_program(g, core, T, topo):
         ny += 16
     Y.wait_ge(S.sty, ny)
 
+    g.iota(T.val[:, 0, 0:512], [[1, 512]], int(OFF) - 1, 0, allow_small_or_imprecise_dtypes=True).then_inc(S.io0a, 1)
     g.wait_ge(S.ones, 1)
-    for e, sel in enumerate((T.sel0, T.sel1)):
-        g.affine_select(sel[:], T.ones[:], [[-1, 16], [0, 8]], Alu.is_equal, 0.0, -(32 * q + 16 * e), 1).then_inc(S.gsel, 1)
-    g.affine_select(T.sh[:], T.ones[:], [[-1, 128]], Alu.is_equal, 0.0, 1, 1).then_inc(S.gsh, 1)
+    g.affine_select(T.sel[0:16, :], T.ones[0:16, :], [[-1, 16], [0, 8]], Alu.is_equal, 0.0, 0, 1).then_inc(S.gsel, 1)
     left = 0
-    g.wait_ge(S.copied, 16)
+    g.wait_ge(S.copied, 32)
     trs = []
     for n, ((r, e), c) in enumerate(sorted(hel.items())):
         eng = topo.engines(core, c)
@@ -208,6 +225,7 @@ def rank_program(g, core, T, topo):
                                      src=T.xd[2 * r + e], dst=T.rin[:]))
         left += k
     g.remote_dma_fused(trs, local_sem=S.left)
+    g.wait_ge(S.copiedn, 16)
     for r in near:
         c = T.cores[r]
         eng = topo.engines(core, c)
@@ -218,10 +236,15 @@ def rank_program(g, core, T, topo):
                for e in range(2)]
         g.remote_dma_fused(trs, local_sem=S.left)
         left += 2 * k
-    g.affine_select(T.wr[:], T.ones[:], [[-8, 16], [1000, 8]], Alu.is_equal, 0.0, -7, 1).then_inc(S.gshw, 1)
+    if q == 0:
+        g.sem_inc(S.sent, 1)
+    g.affine_select(T.eye[:], T.ones[:], [[-1, 128]], Alu.is_equal, 0.0, 0, 1).then_inc(S.geye, 1)
+    g.affine_select(T.sh[:], T.ones[:], [[-1, 128]], Alu.is_equal, 0.0, 1, 1).then_inc(S.gsh, 1)
+    g.affine_select(T.wr[:], T.ones[:], [[-8, 16], [1000, 8]], Alu.is_equal, 0.0, -7, 1).then_inc(S.gwr, 1)
     g.wait_ge(S.gsh, 1)
     g.iota(T.sh[:, 0:128:8], [[0, 16]], 0, 0, allow_small_or_imprecise_dtypes=True).then_inc(S.gshw, 1)
-    for r in range(4):
+    g.iota(T.tabv[:, BY_V:BY_V + BY_G], [[0, BY_G]], int(NONE), 0, allow_small_or_imprecise_dtypes=True).then_inc(S.gfill, 1)
+    for r in range(1, 4):
         g.iota(T.val[:, r, 0:2048], [[0, 4], [1, 512]], 512 * r - 1 + int(OFF), 0,
                allow_small_or_imprecise_dtypes=True).then_inc(io[r], 1)
     for row in range(2):
@@ -255,16 +278,26 @@ def rank_program(g, core, T, topo):
         left += len(topo.engines(core, c))
     g.wait_ge(S.left, left)
 
-    P.wait_ge(S.gsel, 2)
+    P.wait_ge(S.gsel, 1)
     P.wait_ge(S.hcf, 1)
-    P.matmul(T.phc[:, 0:2], T.sel0[:], T.hcf[:], True, True).then_inc(S.hcp, 1)
-    P.matmul(T.phc[:, 2:4], T.sel1[:], T.hcf[:], True, True).then_inc(S.hcp, 1)
-    P.wait_ge(S.gshw, 2)
-    for r0, r1, pb, c1, done in ((0, 1, T.pb0, S.c1a, S.pba), (1, 4, T.pb1, S.c1b, S.pbb)):
+    P.matmul(T.phc[:, 0:4], T.sel[0:16, :], T.hcf[0:16, :], True, True).then_inc(S.hcp, 1)
+    P.wait_ge(S.gshw, 1)
+    P.wait_ge(S.diag, 4)
+    for r0, r1, pb, pm, c1, pbdone, before, pmdone in ((0, 1, T.pb0, T.pm0, S.c1a, S.pba, S.bfa, S.pma),
+                                                       (1, 4, T.pb1, T.pm1, S.c1b, S.pbb, S.bfb, S.pmb)):
         P.wait_ge(c1, 1)
         n = 2 * (r1 - r0)
-        P.matmul(pb[:, 0:n], T.sh[:], T.xf[:, 2 * r0 + 2:2 * r1 + 2, 63], True, False)
-        P.matmul(pb[:, 0:n], T.wr[:], T.xf[:, 2 * r0:2 * r1, 63], False, True).then_inc(done, 1)
+        mm = P.matmul(pb[:, 0:n], T.sh[:], T.xf[:, 2 * r0 + 2:2 * r1 + 2, 67], True, r0 == 0)
+        if r0:
+            P.wait_ge(S.gwr, 1)
+            mm = P.matmul(pb[:, 0:n], T.wr[:], T.xf[:, 2 * r0:2 * r1, 67], False, True)
+        mm.then_inc(pbdone, 1)
+        for e in range(2):
+            out = pm[:, 4 * r0:4 * r1, 16 * e:16 * e + 16]
+            P.matmul(out, T.diag[:, 2 * e + 1, :], T.xf[:, 2 * r0 + 2 + e:2 * r1 + 2:2, 4:68], True, False)
+            if e == 0:
+                P.wait_ge(before, 1)
+            P.matmul(out, T.diag[:, 2 * e, :], T.xf[:, 2 * r0 + 2 + e:2 * r1 + 2:2, 3:67], False, True).then_inc(pmdone, 1)
     P.wait_ge(S.glift, 2)
     for U in range(28, 32):
         wv, half = (U - 28) // 2, U % 2
@@ -288,8 +321,8 @@ def rank_program(g, core, T, topo):
             if U > 0:
                 for s in chains:
                     E.wait_ge(ch[s], 2 * U - 1)
-                    gather(got_at(s, U), tabs[s][:].indirect(offsets(s, U))).then_inc(ch[s], 1)
-                    between(U)
+                    gather(got_at(s, U), tabs[s].indirect(offsets(s, U))).then_inc(ch[s], 1)
+                    between()
             if U < 31:
                 if U % 8 == 7:
                     E.wait_ge(pt[U // 8], 1)
@@ -297,22 +330,26 @@ def rank_program(g, core, T, topo):
                     if U > 0:
                         E.wait_ge(ch[s], 2 * U)
                     c = 512 * s + 64 * (U % 8) + 1
-                    scatter(tabs[s][:].indirect(offsets(s, U)), T.val[:, U // 8, c:c + 64]).then_inc(ch[s], 1)
-                    between(U)
+                    scatter(tabs[s].indirect(offsets(s, U)), T.val[:, U // 8, c:c + 64]).then_inc(ch[s], 1)
+                    between()
 
     A.wait_ge(S.t0a, 1)
-    A.activation(T.tab2[:, 0:512], T.tab0[:, 0:512], Act.Silu).then_inc(S.sfa, 1)
+    A.activation(T.taba[:, 0:128], T.tabv[:, 0:128], Act.Silu).then_inc(S.sfa, 1)
     A.wait_ge(S.t0b, 1)
-    A.activation(T.tab2[:, 512:2560], T.tab0[:, 0:2048], Act.Identity).then_inc(S.sfa, 1)
-    A.activation(T.tab1[:, H - MOVED:H], T.tab0[:, 0:MOVED], Act.Identity).then_inc(S.sfa, 1)
+    A.activation(T.taba[:, 128:1280], T.tabv[:, 0:1152], Act.Identity).then_inc(S.sfa, 1)
+    A.wait_ge(S.t0c, 1)
+    A.activation(T.taba[:, 1280:3328], T.tabv[:, 0:2048], Act.Identity).then_inc(S.sfa, 1)
+    A.activation(T.taba[:, 3328:4352], T.tabv[:, 0:1024], Act.Identity).then_inc(S.sfa, 1)
     A.wait_ge(S.sfa, 3)
-    A.activation(T.tab2[:, 2560:H], T.tab2[:, 0:H - 2560], Act.Identity).then_inc(S.sfc, 1)
-    A.activation(T.tab3[:, 0:2048], T.tab2[:, 0:2048], Act.Identity).then_inc(S.sfc, 1)
-    A.activation(T.tab3[:, 2048:H], T.tab2[:, 0:2048], Act.Identity).then_inc(S.sfc, 1)
-    A.wait_ge(S.sfc, 3)
+    n = (by_a - 4352) // 2
+    for c in (4352, 4352 + n):
+        A.activation(T.taba[:, c:c + n], T.taba[:, 0:n], Act.Identity).then_inc(S.sfc, 1)
+    A.wait_ge(S.sfc, 2)
+    A.wait_ge(S.sfa, 4)
+    A.wait_ge(S.back, back)
     A.wait_ge(S.w0, 1)
     A.wait_ge(rv[0], 32)
-    walk(A, (2, 3), lambda o, i: A.activation(o, i, Act.Identity), lambda o, i: A.activation(o, i, Act.Silu), lambda U: None)
+    walk(A, (2, 3), lambda o, i: A.activation(o, i, Act.Identity), lambda o, i: A.activation(o, i, Act.Silu), lambda: None)
     A.wait_ge(S.rnd2, 1)
     for r in range(N):
         A.dma_start(T.z[32 * r:32 * r + 32, 0:wide], T.ld[64:128, r, 0:wide // 2]).then_inc(S.stz, 16)
@@ -325,39 +362,22 @@ def rank_program(g, core, T, topo):
 
     prep = [0]
 
-    def stages(r0, r1, pb, c1, pbdone, wdone, arr, narr):
-        n = r1 - r0
-
+    def stages(r0, r1, pb, pm, c1, pbdone, bfdone, pmdone, wdone, arr, narr):
         def count(ins):
             ins.then_inc(S.prep, 1)
             prep[0] += 1
 
         def tokens():
             V.wait_ge(arr, narr)
-            V.tensor_scalar(T.xf[:, 2 * r0 + 2:2 * r1 + 2, :], T.land[:, 2 * r0:2 * r1, :], OFF, None, Alu.add).then_inc(c1, 1)
+            V.tensor_scalar(T.xf[:, 2 * r0 + 2:2 * r1 + 2, 4:68], T.land[:, 2 * r0:2 * r1, :], OFF, None, Alu.add).then_inc(c1, 1)
 
-        def products():
-            V.wait_ge(c1, 1)
-            for e in range(2):
-                x = T.xf[:, 2 * r0 + 2 + e:2 * r1 + 2:2, :]
-                count(V.tensor_scalar(T.ptb[:, 256 * e + 64 * r0:256 * e + 64 * r1], x, -OFF, T.hcs[:, 2 * e + 1:2 * e + 2], Alu.add, Alu.mult))
-                count(V.tensor_scalar(T.ta[:, 4 * e + r0:4 * e + r1, 1:64], T.xf[:, 2 * r0 + 2 + e:2 * r1 + 2:2, 0:63],
-                                      -OFF, T.hcs[:, 2 * e:2 * e + 1], Alu.add, Alu.mult))
-
-        def firsts():
+        def before():
             V.wait_ge(pbdone, 1)
-            for e in range(2):
-                count(V.tensor_scalar(T.ta[:, 4 * e + r0:4 * e + r1, 0], pb[:, e:2 * n:2], -OFF, T.hcs[:, 2 * e:2 * e + 1], Alu.add, Alu.mult))
-
-        def sums():
-            V.wait_ge(S.prep, prep[0])
-            for e in range(2):
-                count(V.tensor_tensor(T.mix[:, 4 * r0:4 * r1, 16 * e:16 * e + 16], T.ta[:, 4 * e + r0:4 * e + r1, :],
-                                      T.ptb[:, 256 * e + 64 * r0:256 * e + 64 * r1], Alu.add))
+            V.tensor_scalar(T.xf[:, 2 * r0 + 2:2 * r1 + 2, 3], pb[:, 0:2 * (r1 - r0)], OFF, None, Alu.max).then_inc(bfdone, 1)
 
         def turn():
-            V.wait_ge(S.prep, prep[0])
-            count(V.transpose(T.turn[:, 4 * r0:4 * r1, :], T.mix[:, 4 * r0:4 * r1, :]))
+            V.wait_ge(pmdone, 2)
+            count(V.transpose(T.turn[:, 4 * r0:4 * r1, :], pm[:, 4 * r0:4 * r1, :]))
 
         def whole():
             V.wait_ge(S.prep, prep[0])
@@ -373,7 +393,7 @@ def rank_program(g, core, T, topo):
             V.wait_ge(S.prep, prep[0])
             V.tensor_copy(T.w[:, 128 * r0:128 * r1], T.ki[:, 128 * r0:128 * r1]).then_inc(wdone, 1)
 
-        return [tokens, products, firsts, sums, turn, whole, key, narrow]
+        return [tokens, before, turn, whole, key, narrow]
 
     def seam(r):
         V.wait_ge(rv[r + 1], 32)
@@ -381,46 +401,57 @@ def rank_program(g, core, T, topo):
             V.wait_ge(pt[r - 1], 1)
         V.tensor_copy(T.val[:, r, 512:2049:512], T.val[:, r + 1, 0:2048:512]).then_inc(pt[r], 1)
 
-    first = stages(0, 1, T.pb0, S.c1a, S.pba, S.w0, S.arr0, arr0)
-    rest = stages(1, 4, T.pb1, S.c1b, S.pbb, S.w1, S.arr1, arr1)
-    early = q == 0 or 0 in near
+    def rounded(half):
+        V.wait_ge((S.px0, S.px1)[half], 1)
+        V.tensor_scalar(T.sndf[:, 64 * half:64 * half + 64], (T.px0, T.px1)[half][:, 0:64], MAGIC - OFF, MAGIC,
+                        Alu.add, Alu.subtract).then_inc(S.rnd, 1)
 
+    first = stages(0, 1, T.pb0, T.pm0, S.c1a, S.pba, S.bfa, S.pma, S.w0, S.arr0, arr0)
+    rest = stages(1, 4, T.pb1, T.pm1, S.c1b, S.pbb, S.bfb, S.pmb, S.w1, S.arr1, arr1)
+    filled = [2048, 0]
+
+    def fill(n):
+        V.memset(T.tabv[:, filled[0]:filled[0] + n], NONE).then_inc(S.vfill, 1)
+        filled[0] += n
+        filled[1] += 1
+
+    V.memset(T.tabv[:, 0:128], NONE).then_inc(S.t0a, 1)
     V.memset(T.ones[:], 1.0).then_inc(S.ones, 1)
-    V.memset(T.tab0[:, 0:512], NONE).then_inc(S.t0a, 1)
-    V.memset(T.tab0[:, 512:2048], NONE).then_inc(S.t0b, 1)
-    V.memset(T.xf[:, 0:2, :], OFF).then_inc(S.vinit, 1)
+    V.memset(T.tabv[:, 128:1152], NONE).then_inc(S.t0b, 1)
+    V.memset(T.tabv[:, 1152:2048], NONE).then_inc(S.t0c, 1)
     V.memset(T.got[:, 0:4, 0:64], NONE).then_inc(S.vinit, 1)
     V.memset(T.lift[:, 128:136], 0.0).then_inc(S.vinit, 1)
-    V.memset(T.tab0[:, 2048:H], NONE).then_inc(S.vinit, 1)
-    V.wait_ge(S.hcin, 16)
-    V.tensor_copy(T.hcf[:], T.hci[:]).then_inc(S.hcf, 1)
-    V.memset(T.tab1[:, 0:2048], NONE).then_inc(S.vinit, 1)
-    V.wait_ge(S.hcp, 2)
-    V.tensor_copy(T.hcs[:], T.phc[:, 0:4]).then_inc(S.hcs, 1)
-    V.wait_ge(S.vinit, 5)
-    if early:
-        first[0]()
-    V.memset(T.tab1[:, 2048:H - MOVED], NONE).then_inc(S.sfb, 1)
-    if not early:
-        first[0]()
-    V.wait_ge(S.hcs, 1)
-    for step in first[1:]:
+    V.wait_ge(S.hcin, 32)
+    V.tensor_copy(T.hcf[0:16, :], T.hci[0:16, :, :]).then_inc(S.hcf, 1)
+    fill(2048)
+    V.wait_ge(S.hcp, 1)
+    V.wait_ge(S.geye, 1)
+    for j in range(4):
+        V.tensor_scalar(T.diag[:, j, :], T.eye[:], T.phc[:, j:j + 1], None, Alu.mult).then_inc(S.diag, 1)
+    fill(BY_V - filled[0] - sum(gap))
+    V.wait_ge(S.vinit, 2)
+    for step, n in zip(first, gap):
         step()
-    V.wait_ge(S.sfb, 1)
-    V.wait_ge(S.sfa, 3)
+        if n:
+            fill(n)
+    V.wait_ge(S.vfill, filled[1])
+    V.wait_ge(S.sfa, 4)
+    V.wait_ge(S.back, back)
+    V.wait_ge(S.gfill, 1)
     V.wait_ge(S.w0, 1)
     V.wait_ge(rv[0], 32)
-    seams = [0, 1, 2]
+    extra = dict(zip(REST, rest))
+    for r, n in enumerate(SEAMS):
+        extra[n] = lambda r=r: seam(r)
+    extra[121] = lambda: rounded(0)
+    calls = [0]
 
-    def between(U):
-        if rest:
-            rest.pop(0)()
-        elif seams and U >= (3, 12, 20)[seams[0]]:
-            seam(seams.pop(0))
+    def between():
+        if calls[0] in extra:
+            extra[calls[0]]()
+        calls[0] += 1
 
     walk(V, (0, 1), V.tensor_copy, V.tensor_copy, between)
-    for half, (px, sem) in enumerate(((T.px0, S.px0), (T.px1, S.px1))):
-        V.wait_ge(sem, 1)
-        V.tensor_scalar(T.sndf[:, 64 * half:64 * half + 64], px[:, 0:64], MAGIC - OFF, MAGIC, Alu.add, Alu.subtract).then_inc(S.rnd, 1)
+    rounded(1)
     V.wait_ge(S.ldin, ldin)
     V.tensor_scalar(T.ld[:, :, 0:wide // 2], T.ld[:, :, 0:wide // 2], MAGIC - OFF, MAGIC, Alu.add, Alu.subtract).then_inc(S.rnd2, 1)

from concourse.bass import DstId, RemoteDMATransfer
from concourse.mybir import AluOpType, ActivationFunctionType

OFF = 512.0
NONE = OFF - 1.0
MAGIC = 12582912.0
H = 4096
BY_V, BY_G = 6400, 1024
BY_A = (7168, 2 * H)
GAP = ((384, 768, 256, 256, 256, 256), (384, 768, 0, 0, 0, 0))
REST = (0, 4, 20, 21, 22, 23)
SEAMS = (24, 56, 88)

SCRATCH = {
    "xd": ("dram", [8, 128, 64], "int32"),
    "rin": ("dram", [128, 64], "int32"),
    "rfull": ("dram", [128, 256], "float32"),
    "rhalf": ("dram", [128, 128], "float32"),
    "rfin": ("dram", [128, 128], "float32"),
    "snd": ("dram", [3, 128, 256], "float32"),
    "sndh": ("dram", [128, 128], "float32"),
    "ldf": ("dram", [3, 128, 128], "float32"),
    "land": ("sbuf", [128, 8, 64], "int32"),
    "xf": ("sbuf", [128, 10, 68], "float32"),
    "turn": ("sbuf", [128, 16, 32], "float32"),
    "ki": ("sbuf", [128, 512], "int32"),
    "w": ("sbuf", [128, 512], "uint16"),
    "hci": ("sbuf", [128, 2, 2], "int32"),
    "hcf": ("sbuf", [128, 4], "float32"),
    "ones": ("sbuf", [128, 128], "float32"),
    "sh": ("sbuf", [128, 128], "float32"),
    "wr": ("sbuf", [128, 128], "float32"),
    "sel": ("sbuf", [128, 128], "float32"),
    "eye": ("sbuf", [128, 128], "float32"),
    "diag": ("sbuf", [128, 4, 128], "float32"),
    "lift": ("sbuf", [128, 136], "float32"),
    "tabv": ("sbuf", [128, 2 * H], "float32"),
    "taba": ("sbuf", [128, 2 * H], "float32"),
    "val": ("sbuf", [128, 4, 2064], "float32"),
    "got": ("sbuf", [128, 16, 512], "float32"),
    "ld": ("sbuf", [128, 4, 256], "float32"),
    "sndf": ("sbuf", [128, 128], "float32"),
    "phc": ("psum", [128, 512], "float32"),
    "pb0": ("psum", [128, 512], "float32"),
    "pb1": ("psum", [128, 512], "float32"),
    "pm0": ("psum", [128, 16, 32], "float32"),
    "pm1": ("psum", [128, 16, 32], "float32"),
    "px0": ("psum", [128, 512], "float32"),
    "px1": ("psum", [128, 512], "float32"),
}
SEMAPHORES = ["copied", "copiedn", "sent", "gwr", "hcin", "arr0", "arr1", "left", "rl_in", "rl_full", "rl_half", "rl_fin",
              "ones", "t0a", "t0b", "t0c", "back", "gfill", "io0a", "vinit", "vfill", "hcf", "hcp", "diag", "sfa", "sfc",
              "gsel", "geye", "gsh", "gshw", "glift", "io0", "io1", "io2", "io3", "pt0", "pt1", "pt2",
              "c1a", "c1b", "pba", "pbb", "bfa", "bfb", "pma", "pmb", "prep", "w0", "w1", "rv0", "rv1", "rv2", "rv3",
              "ch0", "ch1", "ch2", "ch3", "out0", "out1", "out2", "out3", "ldin", "ldfin",
              "px0", "px1", "rnd", "rnd2", "sty", "stz"]


def bits(engines):
    m = 0
    for e in engines:
        m |= 1 << e
    return m


def helpers(T, topo, r):
    me = T.cores[r]
    far = [q for q in range(len(T.cores)) if q != r and not topo.may_write(me, T.cores[q])]
    able = [c for c in topo.cores_of(me) if T.rank_of(c) is None and all(topo.may_write(c, T.cores[q]) for q in far)]
    able.sort(key=lambda c: (topo.die(c) != topo.die(me), c))
    out = {}
    for e in range(2):
        for n, q in enumerate(far):
            out[(q, e)] = able[e * len(far) + n]
    return out


def helper_program(g, core, T, topo, r, q, e):
    S = T.sem
    dst = T.cores[q]
    rid, pid = topo.addr(dst, core)
    m = topo.mask(core, dst)
    n = len(topo.engines(core, dst))
    chip = len(topo.engines(T.cores[r], core))
    g.wait_ge(S.rl_in, chip // 8)
    g.remote_dma(T.land[:, 2 * r + e, :], T.rin[:], S.arr0 if r == 0 else S.arr1, S.left, pid, rid, m)
    sent = n
    if e == 0:
        if q < 3:
            g.wait_ge(S.rl_full, chip // 2)
            g.remote_dma(T.ld[:, r, :], T.rfull[:], S.ldin, S.left, pid, rid, m)
            sent += n
        else:
            g.wait_ge(S.rl_half, chip // 2)
            g.remote_dma(T.ld[:, r, 0:128], T.rhalf[:], S.ldin, S.left, pid, rid, m)
            g.wait_ge(S.rl_fin, chip)
            g.remote_dma(T.ldf[r], T.rfin[:], S.ldfin, S.left, pid, rid, m)
            sent += 2 * n
    g.wait_ge(S.left, sent)


def rank_program(g, core, T, topo):
    N = len(T.cores)
    rank = T.rank_of(core)
    if rank is None:
        for r in range(N):
            for (q, e), c in helpers(T, topo, r).items():
                if c == core:
                    helper_program(g, core, T, topo, r, q, e)
        return
    S = T.sem
    V, A, P, Y = g.vector, g.scalar, g.tensor, g.sync
    q = rank
    hel = helpers(T, topo, q)
    near = [r for r in range(N) if r != q and (r, 0) not in hel]
    Alu, Act = AluOpType, ActivationFunctionType
    tabs = [T.tabv[:, 0:H], T.tabv[:, H:2 * H], T.taba[:, 0:H], T.taba[:, H:2 * H]]
    ch = [S.ch0, S.ch1, S.ch2, S.ch3]
    rv = [S.rv0, S.rv1, S.rv2, S.rv3]
    io = [S.io0, S.io1, S.io2, S.io3]
    pt = [S.pt0, S.pt1, S.pt2]
    outs = [S.out0, S.out1, S.out2, S.out3]

    def lands(r):
        src = T.cores[r] if topo.may_write(T.cores[r], core) else helpers(T, topo, r)[(q, 0)]
        return len(topo.engines(src, core))

    def slots_in(r):
        if r == q:
            return 32
        return lands(r) if topo.may_write(T.cores[r], core) else 2 * lands(r)

    def got_at(s, U):
        r, u = U // 8, U % 8
        if r < 3:
            return T.got[:, 4 * r + s, 64 * u:64 * u + 64]
        c = 256 * (s % 2) + 64 * (u % 4)
        return T.got[:, 12 + 2 * (u // 4) + s // 2, c:c + 64]

    late = 0 if q == 0 or 0 in near else 1
    gap, by_a = GAP[late], BY_A[late]
    back = 32 if by_a < 2 * H else 16
    arr0 = slots_in(0)
    arr1 = sum(slots_in(r) for r in range(1, N))
    ldin = 64 + sum(lands(r) for r in range(N) if r != q)

    far = [r for r in range(N) if (r, 0) in hel]
    for E, r in zip((Y, A), far):
        E.dma_start(T.xd[2 * r:2 * r + 2], T.x[32 * r:32 * r + 32, :]).then_inc(S.copied, 16)
    for r in near:
        Y.dma_start(T.xd[2 * r:2 * r + 2], T.x[32 * r:32 * r + 32, :]).then_inc(S.copiedn, 16)
    for e in range(2):
        Y.dma_start(T.hci[0:16, e, :], T.hc[32 * q + 16 * e:32 * q + 16 * e + 16, :]).then_inc(S.hcin, 16)
    for e in range(2):
        Y.dma_start(T.land[:, 2 * q + e, :], T.x[32 * q + 16 * e:32 * q + 16 * e + 16, :]).then_inc(S.arr0 if q == 0 else S.arr1, 16)

    def tokens_to_rows(r):
        Y.wait_ge(io[r], 1 if r else 48)
        for e in range(2):
            Y.dma_start(T.val[16 * e + 8:128:32, r, 0:2048], T.xf[:, 2 * r + 2 + e, 4:68]).then_inc(rv[r], 16)

    def answers_out(r):
        runs = 8 if r < 3 else 4
        for s in range(4):
            Y.wait_ge(ch[s], 2 * (8 * r + runs - 1))
        for row in range(2):
            for e in range(2):
                a0 = 64 * row + 32 * e
                src = T.got[16 * e + 8 * row:128:32, 4 * r:4 * r + runs // 2, :]
                if r == q:
                    Y.dma_start(T.ld[a0:a0 + 32, q, 0:32 * runs], src).then_inc(S.ldin, 16)
                elif r < 3:
                    Y.dma_start(T.snd[r, a0:a0 + 32, :], src).then_inc(outs[r], 16)
                else:
                    Y.dma_start(T.sndh[a0:a0 + 32, :], src).then_inc(outs[r], 16)

    if q == 0:
        Y.wait_ge(S.sent, 1)
    Y.wait_ge(S.io0a, 1)
    for s in range(1, 4):
        Y.dma_start(T.val[:, 0, 512 * s:512 * s + 512], T.val[:, 0, 0:512]).then_inc(io[0], 16)
    Y.wait_ge(S.t0c, 1)
    if by_a < 2 * H:
        Y.dma_start(T.taba[:, by_a:2 * H], T.tabv[:, 0:2 * H - by_a]).then_inc(S.back, 16)
    Y.dma_start(T.tabv[:, BY_V + BY_G:2 * H], T.tabv[:, 0:2 * H - BY_V - BY_G]).then_inc(S.back, 16)
    Y.wait_ge(S.c1a, 1)
    tokens_to_rows(0)
    Y.wait_ge(S.c1b, 1)
    tokens_to_rows(1)
    tokens_to_rows(2)
    answers_out(0)
    tokens_to_rows(3)
    for r in range(1, 4):
        answers_out(r)
    wide = 512 if q < 3 else 256
    ny = nz = 0
    if q == 3:
        Y.wait_ge(S.rnd, 2)
        Y.dma_start(T.y[96:128, 256:512], T.sndf[0:64, :]).then_inc(S.sty, 16)
        Y.dma_start(T.z[96:128, 256:512], T.sndf[64:128, :]).then_inc(S.sty, 16)
        ny += 32
    Y.wait_ge(S.rnd2, 1)
    for r in range(N):
        Y.dma_start(T.y[32 * r:32 * r + 32, 0:wide], T.ld[0:64, r, 0:wide // 2]).then_inc(S.sty, 16)
        ny += 16
    fin = sum(lands(r) for r in range(3)) if q == 3 else 0
    if q == 3:
        Y.wait_ge(S.ldfin, fin)
        Y.dma_start(T.y[0:96, 256:512], T.ldf[:, 0:64, :]).then_inc(S.sty, 16)
        ny += 16
    Y.wait_ge(S.sty, ny)

    g.iota(T.val[:, 0, 0:512], [[1, 512]], int(OFF) - 1, 0, allow_small_or_imprecise_dtypes=True).then_inc(S.io0a, 1)
    g.wait_ge(S.ones, 1)
    g.affine_select(T.sel[0:16, :], T.ones[0:16, :], [[-1, 16], [0, 8]], Alu.is_equal, 0.0, 0, 1).then_inc(S.gsel, 1)
    left = 0
    g.wait_ge(S.copied, 32)
    trs = []
    for n, ((r, e), c) in enumerate(sorted(hel.items())):
        eng = topo.engines(core, c)
        k = len(eng) // 8
        use = eng[len(eng) // 2 + n * k:len(eng) // 2 + (n + 1) * k]
        rid, pid = topo.addr(c, core)
        trs.append(RemoteDMATransfer(dst_ids=[DstId(rid=rid, pnc=pid)], dma_engine_mask=bits(use), remote_sem=S.rl_in,
                                     src=T.xd[2 * r + e], dst=T.rin[:]))
        left += k
    g.remote_dma_fused(trs, local_sem=S.left)
    g.wait_ge(S.copiedn, 16)
    for r in near:
        c = T.cores[r]
        eng = topo.engines(core, c)
        k = len(eng) // 2
        rid, pid = topo.addr(c, core)
        trs = [RemoteDMATransfer(dst_ids=[DstId(rid=rid, pnc=pid)], dma_engine_mask=bits(eng[e * k:(e + 1) * k]),
                                 remote_sem=S.arr0 if q == 0 else S.arr1, src=T.xd[2 * r + e], dst=T.land[:, 2 * q + e, :])
               for e in range(2)]
        g.remote_dma_fused(trs, local_sem=S.left)
        left += 2 * k
    if q == 0:
        g.sem_inc(S.sent, 1)
    g.affine_select(T.eye[:], T.ones[:], [[-1, 128]], Alu.is_equal, 0.0, 0, 1).then_inc(S.geye, 1)
    g.affine_select(T.sh[:], T.ones[:], [[-1, 128]], Alu.is_equal, 0.0, 1, 1).then_inc(S.gsh, 1)
    g.affine_select(T.wr[:], T.ones[:], [[-8, 16], [1000, 8]], Alu.is_equal, 0.0, -7, 1).then_inc(S.gwr, 1)
    g.wait_ge(S.gsh, 1)
    g.iota(T.sh[:, 0:128:8], [[0, 16]], 0, 0, allow_small_or_imprecise_dtypes=True).then_inc(S.gshw, 1)
    g.iota(T.tabv[:, BY_V:BY_V + BY_G], [[0, BY_G]], int(NONE), 0, allow_small_or_imprecise_dtypes=True).then_inc(S.gfill, 1)
    for r in range(1, 4):
        g.iota(T.val[:, r, 0:2048], [[0, 4], [1, 512]], 512 * r - 1 + int(OFF), 0,
               allow_small_or_imprecise_dtypes=True).then_inc(io[r], 1)
    for row in range(2):
        g.affine_select(T.lift[:, 64 * row:64 * row + 64], T.ones[:, 0:64], [[-16, 2], [-32, 4], [1000, 8]],
                        Alu.is_equal, 0.0, -8 * row - 7000, 1).then_inc(S.glift, 1)
    for r in range(4):
        if r == q:
            continue
        g.wait_ge(outs[r], 64)
        src = T.snd[r] if r < 3 else T.sndh[:]
        if r in near:
            c = T.cores[r]
            rid, pid = topo.addr(c, core)
            g.remote_dma(T.ld[:, q, :] if r < 3 else T.ld[:, q, 0:128], src, S.ldin, S.left, pid, rid, topo.mask(core, c))
            left += len(topo.engines(core, c))
        else:
            c = hel[(r, 0)]
            eng = topo.engines(core, c)
            use = eng[len(eng) // 2:]
            rid, pid = topo.addr(c, core)
            g.remote_dma(T.rfull[:] if r < 3 else T.rhalf[:], src, S.rl_full if r < 3 else S.rl_half, S.left, pid, rid, bits(use))
            left += len(use)
    if q != 3:
        g.wait_ge(S.rnd, 2)
        c = T.cores[3] if 3 in near else hel[(3, 0)]
        rid, pid = topo.addr(c, core)
        if 3 in near:
            g.remote_dma(T.ldf[q], T.sndf[:], S.ldfin, S.left, pid, rid, topo.mask(core, c))
        else:
            g.remote_dma(T.rfin[:], T.sndf[:], S.rl_fin, S.left, pid, rid, topo.mask(core, c))
        left += len(topo.engines(core, c))
    g.wait_ge(S.left, left)

    P.wait_ge(S.gsel, 1)
    P.wait_ge(S.hcf, 1)
    P.matmul(T.phc[:, 0:4], T.sel[0:16, :], T.hcf[0:16, :], True, True).then_inc(S.hcp, 1)
    P.wait_ge(S.gshw, 1)
    P.wait_ge(S.diag, 4)
    for r0, r1, pb, pm, c1, pbdone, before, pmdone in ((0, 1, T.pb0, T.pm0, S.c1a, S.pba, S.bfa, S.pma),
                                                       (1, 4, T.pb1, T.pm1, S.c1b, S.pbb, S.bfb, S.pmb)):
        P.wait_ge(c1, 1)
        n = 2 * (r1 - r0)
        mm = P.matmul(pb[:, 0:n], T.sh[:], T.xf[:, 2 * r0 + 2:2 * r1 + 2, 67], True, r0 == 0)
        if r0:
            P.wait_ge(S.gwr, 1)
            mm = P.matmul(pb[:, 0:n], T.wr[:], T.xf[:, 2 * r0:2 * r1, 67], False, True)
        mm.then_inc(pbdone, 1)
        for e in range(2):
            out = pm[:, 4 * r0:4 * r1, 16 * e:16 * e + 16]
            P.matmul(out, T.diag[:, 2 * e + 1, :], T.xf[:, 2 * r0 + 2 + e:2 * r1 + 2:2, 4:68], True, False)
            if e == 0:
                P.wait_ge(before, 1)
            P.matmul(out, T.diag[:, 2 * e, :], T.xf[:, 2 * r0 + 2 + e:2 * r1 + 2:2, 3:67], False, True).then_inc(pmdone, 1)
    P.wait_ge(S.glift, 2)
    for U in range(28, 32):
        wv, half = (U - 28) // 2, U % 2
        px = (T.px0, T.px1)[half]
        for n, s in enumerate((0, 2, 1, 3)):
            P.wait_ge(ch[s], 2 * U)
            j = 2 * s + wv
            last = wv == 1 and n == 3
            mm = P.matmul(px[:, 0:64], T.lift[:, 7 - j:135 - j], got_at(s, U), wv == 0 and n == 0, last)
            if last:
                mm.then_inc((S.px0, S.px1)[half], 1)

    def offsets(s, U):
        c = 128 * (U // 8) + 4 * (8 * s + U % 8)
        return T.w[:, c:c + 4]

    def walk(E, chains, gather, scatter, between):
        for U in range(32):
            if U == 8:
                E.wait_ge(S.w1, 1)
            if U > 0:
                for s in chains:
                    E.wait_ge(ch[s], 2 * U - 1)
                    gather(got_at(s, U), tabs[s].indirect(offsets(s, U))).then_inc(ch[s], 1)
                    between()
            if U < 31:
                if U % 8 == 7:
                    E.wait_ge(pt[U // 8], 1)
                for s in chains:
                    if U > 0:
                        E.wait_ge(ch[s], 2 * U)
                    c = 512 * s + 64 * (U % 8) + 1
                    scatter(tabs[s].indirect(offsets(s, U)), T.val[:, U // 8, c:c + 64]).then_inc(ch[s], 1)
                    between()

    A.wait_ge(S.t0a, 1)
    A.activation(T.taba[:, 0:128], T.tabv[:, 0:128], Act.Silu).then_inc(S.sfa, 1)
    A.wait_ge(S.t0b, 1)
    A.activation(T.taba[:, 128:1280], T.tabv[:, 0:1152], Act.Identity).then_inc(S.sfa, 1)
    A.wait_ge(S.t0c, 1)
    A.activation(T.taba[:, 1280:3328], T.tabv[:, 0:2048], Act.Identity).then_inc(S.sfa, 1)
    A.activation(T.taba[:, 3328:4352], T.tabv[:, 0:1024], Act.Identity).then_inc(S.sfa, 1)
    A.wait_ge(S.sfa, 3)
    n = (by_a - 4352) // 2
    for c in (4352, 4352 + n):
        A.activation(T.taba[:, c:c + n], T.taba[:, 0:n], Act.Identity).then_inc(S.sfc, 1)
    A.wait_ge(S.sfc, 2)
    A.wait_ge(S.sfa, 4)
    A.wait_ge(S.back, back)
    A.wait_ge(S.w0, 1)
    A.wait_ge(rv[0], 32)
    walk(A, (2, 3), lambda o, i: A.activation(o, i, Act.Identity), lambda o, i: A.activation(o, i, Act.Silu), lambda: None)
    A.wait_ge(S.rnd2, 1)
    for r in range(N):
        A.dma_start(T.z[32 * r:32 * r + 32, 0:wide], T.ld[64:128, r, 0:wide // 2]).then_inc(S.stz, 16)
        nz += 16
    if q == 3:
        A.wait_ge(S.ldfin, fin)
        A.dma_start(T.z[0:96, 256:512], T.ldf[:, 64:128, :]).then_inc(S.stz, 16)
        nz += 16
    A.wait_ge(S.stz, nz)

    prep = [0]

    def stages(r0, r1, pb, pm, c1, pbdone, bfdone, pmdone, wdone, arr, narr):
        def count(ins):
            ins.then_inc(S.prep, 1)
            prep[0] += 1

        def tokens():
            V.wait_ge(arr, narr)
            V.tensor_scalar(T.xf[:, 2 * r0 + 2:2 * r1 + 2, 4:68], T.land[:, 2 * r0:2 * r1, :], OFF, None, Alu.add).then_inc(c1, 1)

        def before():
            V.wait_ge(pbdone, 1)
            V.tensor_scalar(T.xf[:, 2 * r0 + 2:2 * r1 + 2, 3], pb[:, 0:2 * (r1 - r0)], OFF, None, Alu.max).then_inc(bfdone, 1)

        def turn():
            V.wait_ge(pmdone, 2)
            count(V.transpose(T.turn[:, 4 * r0:4 * r1, :], pm[:, 4 * r0:4 * r1, :]))

        def whole():
            V.wait_ge(S.prep, prep[0])
            for b in range(4):
                count(V.tensor_copy(T.ki[:, 128 * r0 + b:128 * r1:4], T.turn[:, 4 * r0 + b:4 * r1:4, :]))

        def key():
            V.wait_ge(S.prep, prep[0])
            k = T.ki[:, 128 * r0:128 * r1]
            count(V.tensor_scalar(k, k, 9, H - 1, Alu.arith_shift_right, Alu.bitwise_and))

        def narrow():
            V.wait_ge(S.prep, prep[0])
            V.tensor_copy(T.w[:, 128 * r0:128 * r1], T.ki[:, 128 * r0:128 * r1]).then_inc(wdone, 1)

        return [tokens, before, turn, whole, key, narrow]

    def seam(r):
        V.wait_ge(rv[r + 1], 32)
        if r > 0:
            V.wait_ge(pt[r - 1], 1)
        V.tensor_copy(T.val[:, r, 512:2049:512], T.val[:, r + 1, 0:2048:512]).then_inc(pt[r], 1)

    def rounded(half):
        V.wait_ge((S.px0, S.px1)[half], 1)
        V.tensor_scalar(T.sndf[:, 64 * half:64 * half + 64], (T.px0, T.px1)[half][:, 0:64], MAGIC - OFF, MAGIC,
                        Alu.add, Alu.subtract).then_inc(S.rnd, 1)

    first = stages(0, 1, T.pb0, T.pm0, S.c1a, S.pba, S.bfa, S.pma, S.w0, S.arr0, arr0)
    rest = stages(1, 4, T.pb1, T.pm1, S.c1b, S.pbb, S.bfb, S.pmb, S.w1, S.arr1, arr1)
    filled = [2048, 0]

    def fill(n):
        V.memset(T.tabv[:, filled[0]:filled[0] + n], NONE).then_inc(S.vfill, 1)
        filled[0] += n
        filled[1] += 1

    V.memset(T.tabv[:, 0:128], NONE).then_inc(S.t0a, 1)
    V.memset(T.ones[:], 1.0).then_inc(S.ones, 1)
    V.memset(T.tabv[:, 128:1152], NONE).then_inc(S.t0b, 1)
    V.memset(T.tabv[:, 1152:2048], NONE).then_inc(S.t0c, 1)
    V.memset(T.got[:, 0:4, 0:64], NONE).then_inc(S.vinit, 1)
    V.memset(T.lift[:, 128:136], 0.0).then_inc(S.vinit, 1)
    V.wait_ge(S.hcin, 32)
    V.tensor_copy(T.hcf[0:16, :], T.hci[0:16, :, :]).then_inc(S.hcf, 1)
    fill(2048)
    V.wait_ge(S.hcp, 1)
    V.wait_ge(S.geye, 1)
    for j in range(4):
        V.tensor_scalar(T.diag[:, j, :], T.eye[:], T.phc[:, j:j + 1], None, Alu.mult).then_inc(S.diag, 1)
    fill(BY_V - filled[0] - sum(gap))
    V.wait_ge(S.vinit, 2)
    for step, n in zip(first, gap):
        step()
        if n:
            fill(n)
    V.wait_ge(S.vfill, filled[1])
    V.wait_ge(S.sfa, 4)
    V.wait_ge(S.back, back)
    V.wait_ge(S.gfill, 1)
    V.wait_ge(S.w0, 1)
    V.wait_ge(rv[0], 32)
    extra = dict(zip(REST, rest))
    for r, n in enumerate(SEAMS):
        extra[n] = lambda r=r: seam(r)
    extra[121] = lambda: rounded(0)
    calls = [0]

    def between():
        if calls[0] in extra:
            extra[calls[0]]()
        calls[0] += 1

    walk(V, (0, 1), V.tensor_copy, V.tensor_copy, between)
    rounded(1)
    V.wait_ge(S.ldin, ldin)
    V.tensor_scalar(T.ld[:, :, 0:wide // 2], T.ld[:, :, 0:wide // 2], MAGIC - OFF, MAGIC, Alu.add, Alu.subtract).then_inc(S.rnd2, 1)
